import numpy as np
import ml_dtypes


def mxq(x, axis, fmt="e4m3"):
    dtype, down = {"e4m3": (ml_dtypes.float8_e4m3fn, 7), "e5m2": (ml_dtypes.float8_e5m2, 14)}[fmt]
    v = np.moveaxis(np.asarray(x, np.float32).astype(ml_dtypes.bfloat16).astype(np.float64), axis, -1)
    blocks = v.reshape(v.shape[:-1] + (-1, 32))
    amax = np.abs(blocks).max(-1, keepdims=True)
    byte = np.maximum(np.where(amax > 0, np.frexp(amax)[1] - 1 + 127, 0) - down, 1)
    scale = np.exp2(byte - 127.0)
    codes = (blocks / scale).astype(np.float32).astype(dtype).astype(np.float64)
    return np.moveaxis((codes * scale).reshape(v.shape), -1, axis)


WIDE = False


def mx_kscale(k):
    if not WIDE:
        return np.ones(k)
    levels = np.array([10, -10, 5, -5, 0])
    if k % 512:
        return np.exp2(np.random.permutation(np.resize(levels, k // 32))).repeat(32)
    a = np.empty((k // 512, 16))
    for p in range(k // 512):
        a[p, :8] = np.random.permutation(np.resize(levels, 8))
        for g in range(8):
            far = levels[np.abs(levels - a[p, g]) >= 10]
            a[p, g + 8] = far[np.random.randint(len(far))]
    return np.exp2(a.ravel()).repeat(32)


BF16 = ml_dtypes.bfloat16


def bf(x):
    return np.asarray(x, np.float32).astype(BF16)


def f64(x):
    return np.asarray(x).astype(np.float64)


E2M1 = np.array([0.0, 0.5, 1.0, 1.5, 2.0, 3.0, 4.0, 6.0, -0.0, -0.5, -1.0, -1.5, -2.0, -3.0, -4.0, -6.0])


def pack_weight(w, fmt):
    k, n = w.shape
    w = f64(bf(w)).reshape(k // 32, 32, n)
    amax = np.abs(w).max(1)
    if fmt == "e4m3":
        byte = np.frexp(amax)[1] - 1 + 127 - 7
    else:
        mant, ex = np.frexp(amax / 6.0)
        byte = np.where(mant > 0.5, ex, ex - 1) + 127
    byte = np.clip(np.where(amax > 0, byte, 1), 1, 254)
    scaled = (w * np.exp2(127.0 - byte)[:, None, :]).reshape(k, n).astype(np.float32)
    by_word = np.ascontiguousarray(scaled.reshape(k // 512, 128, 4, n).transpose(0, 1, 3, 2))
    if fmt == "e4m3":
        words = by_word.astype(ml_dtypes.float8_e4m3fn).view(np.uint8)
    else:
        c = by_word.astype(ml_dtypes.float4_e2m1fn).view(np.uint8) & 0xF
        words = c[..., 0::2] | (c[..., 1::2] << 4)
    return np.ascontiguousarray(words), np.ascontiguousarray(byte.astype(np.uint8).reshape(k // 512, 16, n))


def unpack_weight(words, scales, fmt):
    g, p, n, _ = words.shape
    if fmt == "e4m3":
        vals = np.ascontiguousarray(words).view(ml_dtypes.float8_e4m3fn).astype(np.float64)
    else:
        nib = np.empty((g, p, n, 4), np.uint8)
        nib[..., 0::2] = words & 0xF
        nib[..., 1::2] = words >> 4
        vals = E2M1[nib]
    vals = vals * np.repeat(np.exp2(scales.astype(np.float64) - 127.0), 8, axis=1)[..., None]
    return vals.transpose(0, 1, 3, 2).reshape(g * 512, n)
def pack4(w):
    words, scales = pack_weight(w, "e2m1")
    return words.reshape(words.shape[0], 128, -1), scales


def unpack4(words, scales):
    return unpack_weight(words.reshape(words.shape[0], 128, -1, 2), scales, "e2m1")


H, W, Z = 1536, 1024, 512

RADIUS = W // 8


def setup_inputs():
    s, v, t = mx_kscale(W), mx_kscale(Z), mx_kscale(H)
    inside = slice(Z // 2, Z // 2 + W)
    cols, rows = np.arange(W + Z) - Z // 2, np.arange(H)
    light = 0.5 * np.sin(2 * np.pi * (rows / H + np.random.rand()))[:, None] + 0.5 * np.sin(2 * np.pi * (cols / W + np.random.rand()))
    scene = np.exp(light + 0.8 * np.random.standard_normal((H, W + Z)))
    across = np.exp(0.5 * np.random.standard_normal((W + Z, W))) / (1 + ((cols[:, None] - np.arange(W)) / RADIUS) ** 2)
    across = across / across.sum(0)
    down = np.exp(0.5 * np.random.standard_normal((H, H))) / (1 + ((rows[:, None] - rows) / RADIUS) ** 2)
    down = down / down.sum(0)
    sens = np.exp(0.2 * np.random.standard_normal(W)) * s
    far_words, far_scales = pack4(np.delete(across, inside, 0) / v[:, None])
    down_words, down_scales = pack4(down / t[:, None])
    return {"tile": bf(scene[:, inside] * sens),
            "halo": bf(np.delete(scene, inside, 1) * v),
            "near": bf(across[inside] / sens[:, None]),
            "far_words": far_words, "far_scales": far_scales,
            "row_weight": bf(np.exp(0.5 * np.random.standard_normal(H)) * t),
            "down_words": down_words, "down_scales": down_scales,
            "col_gain": bf(1 / sens)}


def reference(tile, halo, near, far_words, far_scales, row_weight, down_words, down_scales, col_gain):
    own = mxq(f64(tile), 1, "e4m3") @ mxq(f64(near), 0, "e4m3")
    outer = mxq(f64(halo), 1, "e4m3") @ unpack4(far_words, far_scales)
    h = (own + outer) * f64(row_weight)[:, None]
    surround = unpack4(down_words, down_scales).T @ mxq(h, 0, "e4m3")
    return np.log(f64(tile) * f64(col_gain)) - np.log(surround)

@@ -1,0 +1,356 @@
+from contextlib import ExitStack
+
+import concourse.mybir as mybir
+from concourse.masks import make_identity
+
+H, W, Z = 1536, 1024, 512
+FLOPS = 2 * H * W * (W + Z) + 2 * H * H * W
+
+F32 = mybir.dt.float32
+BF16 = mybir.dt.bfloat16
+I32 = mybir.dt.int32
+U32 = mybir.dt.uint32
+U8 = mybir.dt.uint8
+FP8X4 = mybir.dt.float8_e4m3fn_x4
+FP4X4 = mybir.dt.float4_e2m1fn_x4
+ACT = mybir.ActivationFunctionType
+ALU = mybir.AluOpType
+
+P = 128
+PACK = 4
+K_PASS = P * PACK
+N = 512
+GROUPS = H // K_PASS
+PAIRS = 2 * GROUPS
+ROW_TILES = H // P
+BANKS = 8
+UNITS = 3 * GROUPS
+NEAR_SPLIT = 512
+TURN_BANKS = 3
+GAINS = [0] * 9
+LOGS = [0] * 9
+NEAR_AT = [3, 5]
+LEAD = 5
+AHEAD_AT = 1
+EARLY = 1
+BG = [0, 0, 0, 2]
+EVAC_V = []
+WARM = [12, 8]
+
+
+def tile_single_scale_retinex_s3_kernel(
+    tc, tile, halo, near, far_words, far_scales, row_weight, down_words, down_scales, col_gain, out
+):
+    nc = tc.nc
+    with ExitStack() as ctx:
+        keep = ctx.enter_context(tc.tile_pool(name="keep", bufs=1))
+        psum = ctx.enter_context(tc.psum_pool(name="psum", bufs=1))
+        ctx.enter_context(tc.manual_schedule(engines={mybir.EngineType.PE, mybir.EngineType.SP, mybir.EngineType.Pool}))
+
+        def sbuf(name, shape, dtype):
+            return keep.tile(shape, dtype, name=name, align_bytes=64)
+
+        rings = {}
+
+        def ring(pool, name, depth, shape, dtype):
+            made = rings.setdefault(name, [])
+            made.append(pool.tile(shape, dtype, name="%s%d" % (name, len(made) % depth), align_bytes=64))
+            return made[-1]
+
+        def bank(role, first, count):
+            made = rings.setdefault(role, [])
+            made.append(psum.tile([P, N], F32, name="bank%d" % (first + len(made) % count)))
+            return made[-1]
+
+        def cols(half):
+            return slice(half * N, (half + 1) * N)
+
+        near_rows = near.rearrange("(a p j) c -> a p j c", p=P, j=PACK)
+        tile_rows = tile.rearrange("(j p) c -> p j c", p=P)
+        halo_rows = halo.rearrange("(j p) c -> p j c", p=P)
+
+        ident = sbuf("ident", [P, P], F32)
+        make_identity(nc, ident[:])
+        far_plane = sbuf("far_plane", [P, W], U8)
+        down_plane = sbuf("down_plane", [P, GROUPS * H], U8)
+        one = sbuf("one", [P, 1], F32)
+        warm = sbuf("warm", [P, 1], F32)
+        nc.vector.memset(one[:], 1.0)
+        zeros = sbuf("zeros", [P, PACK * P], BF16)
+        zero_codes = sbuf("zero_codes", [P, P], U32)
+        zero_scales = sbuf("zero_scales", [P, P], U8)
+        nc.vector.memset(zeros[:], 0.0)
+        nc.vector.memset(far_plane[:].bitcast(I32), 0)
+        nc.vector.quantize_mx(out=zero_codes[:].bitcast(FP8X4), scales=zero_scales[:], in_=zeros[:])
+        nc.gpsimd.memset(down_plane[:].bitcast(I32), 0)
+        nc.scalar.activation(out=warm[:], in_=one[:], func=ACT.Ln)
+
+        rows_in, near_in = {}, {}
+
+        def load_unit(n, pieces=1):
+            g, a = divmod(n, 3)
+            src = tile_rows[:, :, cols(a)] if a < 2 else halo_rows
+            per = PACK // pieces
+            for i in range(pieces):
+                j0 = PACK * g + per * i
+                raw = sbuf("rows%d_%d" % (n, i), [P, per, N], BF16)
+                nc.sync.dma_start(out=raw[:], in_=src[:, j0 : j0 + per, :])
+                for j in range(per):
+                    rows_in[j0 + j, a] = raw[:, j, :]
+
+        def load_near(a, half):
+            raw = sbuf("near%d_%d" % (a, half), [P, PACK, N], BF16)
+            nc.sync.dma_start(out=raw[:], in_=near_rows[a][:, :, cols(half)])
+            near_in[a, half] = raw
+
+        far = sbuf("far", [P, 2 * W], U8)
+        down = sbuf("down", [P, GROUPS * 2 * H], U8)
+        weight_raw = sbuf("weight_raw", [P, GROUPS, PACK], BF16)
+        weight = sbuf("weight", [P, GROUPS, PACK], F32)
+        gain_raw = sbuf("gain_raw", [P, 8], BF16)
+        gain_col = sbuf("gain_col", [P, 8], F32)
+        gain = sbuf("gain", [P, W], F32)
+
+        nc.sync.dma_start(out=gain_raw[:], in_=col_gain.rearrange("(n m) -> n m", m=8))
+        load_near(0, 0)
+        load_unit(0)
+        load_unit(1)
+        for q in range(4):
+            nc.sync.dma_start(
+                out=far_plane[32 * q : 32 * q + 4, :].bitcast(I32), in_=far_scales[0][4 * q : 4 * q + 4, :].bitcast(I32)
+            )
+        load_near(1, 0)
+        load_unit(2)
+        nc.sync.dma_start(out=far[:].bitcast(I32), in_=far_words[0].bitcast(I32))
+        nc.sync.dma_start(out=weight_raw[:], in_=row_weight.rearrange("(g p t) -> p g t", p=P, t=PACK))
+        for n in range(3, UNITS):
+            load_unit(n)
+            if n in (5, 6):
+                load_near(n - 5, 1)
+        nc.sync.dma_start(
+            out=down[:].bitcast(I32).rearrange("p (g n) -> p g n", g=GROUPS),
+            in_=down_words.bitcast(I32).rearrange("g p n -> p g n"),
+        )
+        for q in range(4):
+            nc.sync.dma_start(
+                out=down_plane[32 * q : 32 * q + 4, :].bitcast(I32).rearrange("r (g n) -> r g n", g=GROUPS),
+                in_=down_scales.bitcast(I32)[:, 4 * q : 4 * q + 4, :].rearrange("g r n -> r g n"),
+            )
+
+        grouped, mx, turned, sums, rounded, logs, lsur = {}, {}, {}, {}, {}, {}, {}
+
+        def interleave(engine_copy, key, src, c0, c1):
+            engine_copy(
+                out=grouped[key][:, c0:c1, :].rearrange("p (c i) t -> p c t i", i=4),
+                in_=src[:, :, c0:c1].rearrange("p t (c i) -> p c t i", i=4),
+            )
+
+        def quantize(key):
+            src = grouped[key]
+            width = src.shape[1]
+            name = "_".join([str(x) for x in key])
+            codes = sbuf("codes" + name, [P, width], U32)
+            scales = sbuf("scales" + name, [P, width], U8)
+            nc.vector.quantize_mx(out=codes[:].bitcast(FP8X4), scales=scales[:], in_=src[:].rearrange("p c t -> p (c t)"))
+            mx[key] = (codes, scales)
+
+        def near_interleave(a, half, split):
+            key = ("near", a, half)
+            grouped[key] = ring(keep, "wide", 5, [P, N, PACK], BF16)
+            interleave(nc.vector.tensor_copy, key, near_in[a, half], 0, split)
+            if split < N:
+                interleave(nc.scalar.copy, key, near_in[a, half], split, N)
+
+        def transpose(n):
+            g, a = divmod(n, 3)
+            key = ("x", g, a)
+            grouped[key] = ring(keep, "wide", 5, [P, N, PACK], BF16)
+            dst = grouped[key][:].rearrange("p c t -> p (c t)").bitcast(F32)
+            dst = dst.rearrange("p (t j m u) -> p j t m u", t=PACK, j=PACK, u=2)
+            for b in range(2):
+                ps = bank("turn", 0, TURN_BANKS)
+                for i in range(2):
+                    words = rows_in[PACK * g + 2 * b + i, a].bitcast(F32)
+                    for u in range(2):
+                        nc.tensor.transpose(ps[:, (2 * i + u) * P : (2 * i + u + 1) * P], words[:, u : 2 * P : 2], ident[:])
+                (nc.vector.tensor_copy if 2 * n + b in EVAC_V else nc.scalar.copy)(
+                    out=dst[:, 2 * b : 2 * b + 2], in_=ps[:].rearrange("p (j u m t) -> p j t m u", j=2, u=2, t=PACK)
+                )
+
+        def keep_warm(count):
+            ps = psum.tile([P, N], F32, name="bank7")
+            for i in range(count):
+                nc.tensor.matmul_mx(
+                    out=ps[:, (i % 4) * P : (i % 4 + 1) * P],
+                    lhsT=zero_codes[:].bitcast(FP8X4),
+                    lhsT_scale=zero_scales[:],
+                    rhs=zero_codes[:].bitcast(FP8X4),
+                    rhs_scale=zero_scales[:],
+                    start=True,
+                    stop=True,
+                )
+
+        def spread_gain():
+            for b in range(2):
+                ps = bank("turn", 0, TURN_BANKS)
+                for m in range(4):
+                    src = gain_col[:, 4 * b + m : 4 * b + m + 1].to_broadcast([P, P])
+                    nc.tensor.transpose(ps[:, m * P : (m + 1) * P], src, ident[:])
+                nc.vector.tensor_copy(
+                    out=gain[:].rearrange("p (n m) -> p n m", m=8)[:, :, 4 * b : 4 * b + 4],
+                    in_=ps[:].rearrange("p (m n) -> p n m", m=4),
+                )
+
+        def blur_pass(g, t, half, a):
+            if a == 0:
+                sums[g, t, half] = bank("late", 0, BANKS) if half else bank("sum", TURN_BANKS, BANKS - TURN_BANKS)
+            codes, scales = mx["x", g, a]
+            if a < 2:
+                rhs, rhs_scale = mx["near", a, half][0][:].bitcast(FP8X4), mx["near", a, half][1][:]
+            else:
+                rhs, rhs_scale = far[:, 2 * N * half : 2 * N * (half + 1)].bitcast(FP4X4), far_plane[:, cols(half)]
+            nc.tensor.matmul_mx(
+                out=sums[g, t, half][:],
+                lhsT=codes[:, t * P : (t + 1) * P].bitcast(FP8X4),
+                lhsT_scale=scales[:, t * P : (t + 1) * P],
+                rhs=rhs,
+                rhs_scale=rhs_scale,
+                start=(a == 0),
+                stop=(a == 2),
+            )
+
+        def empty_sums(g, t, half):
+            if t == 0:
+                rounded[g, half] = ring(keep, "rounded", 3, [P, PACK, N], BF16)
+            nc.scalar.activation(
+                out=rounded[g, half][:, t, :], in_=sums[g, t, half][:], func=ACT.Copy, scale=weight[:, g, t : t + 1]
+            )
+
+        def h_interleave(g, half):
+            key = ("h", g, half)
+            grouped[key] = ring(keep, "wide", 5, [P, N, PACK], BF16)
+            interleave(nc.vector.tensor_copy, key, rounded[g, half], 0, N)
+
+        def blur_cols(j, half):
+            ps = bank("late", 0, BANKS)
+            for g in range(GROUPS):
+                codes, scales = mx["h", g, half]
+                nc.tensor.matmul_mx(
+                    out=ps[:],
+                    lhsT=down[:, 2 * (g * H + j * P) : 2 * (g * H + (j + 1) * P)].bitcast(FP4X4),
+                    lhsT_scale=down_plane[:, g * H + j * P : g * H + (j + 1) * P],
+                    rhs=codes[:].bitcast(FP8X4),
+                    rhs_scale=scales[:],
+                    start=(g == 0),
+                    stop=(g == GROUPS - 1),
+                )
+            sums["s", j, half] = ps
+
+        def gain_tile(j, half):
+            logs[j, half] = sbuf("log%d_%d" % (j, half), [P, N], F32)
+            nc.vector.tensor_tensor(out=logs[j, half][:], in0=rows_in[j, half], in1=gain[:, cols(half)], op=ALU.mult)
+
+        def log_tile(j, half):
+            nc.scalar.activation(out=logs[j, half][:], in_=logs[j, half][:], func=ACT.Ln)
+
+        def log_surround(j, half):
+            lsur[j, half] = ring(keep, "lsur", 4, [P, N], F32)
+            nc.scalar.activation(out=lsur[j, half][:], in_=sums["s", j, half][:], func=ACT.Ln)
+
+        def finish(j, half):
+            nc.vector.tensor_tensor(out=logs[j, half][:], in0=logs[j, half][:], in1=lsur[j, half][:], op=ALU.subtract)
+            nc.sync.dma_start(out=out[j * P : (j + 1) * P, cols(half)], in_=logs[j, half][:])
+
+        todo = [(j, half) for half in range(2) for j in range(ROW_TILES)]
+        gained, logged = [], []
+
+        def more_gain():
+            if len(gained) < len(todo):
+                gain_tile(*todo[len(gained)])
+                gained.append(1)
+
+        def more_log():
+            if len(logged) < len(gained):
+                log_tile(*todo[len(logged)])
+                logged.append(1)
+
+        keep_warm(WARM[0])
+        nc.vector.tensor_copy(out=gain_col[:], in_=gain_raw[:])
+        spread_gain()
+        keep_warm(WARM[1])
+        transpose(0)
+        keep_warm(WARM[1])
+        near_interleave(0, 0, NEAR_SPLIT)
+        quantize(("x", 0, 0))
+        quantize(("near", 0, 0))
+        transpose(1)
+        more_gain()
+        near_interleave(1, 0, NEAR_SPLIT)
+        quantize(("x", 0, 1))
+        nc.vector.tensor_copy(out=weight[:], in_=weight_raw[:])
+        quantize(("near", 1, 0))
+
+        def blur_right(step):
+            for a in range(3):
+                blur_pass(*divmod(step, PACK), 1, a)
+            empty_sums(*divmod(step, PACK), 1)
+
+        for n in range(UNITS):
+            g, a = divmod(n, 3)
+            if n == UNITS - 1:
+                for step in range(EARLY):
+                    blur_right(step)
+            for t in range(PACK):
+                blur_pass(g, t, 0, a)
+                if a == 2:
+                    empty_sums(g, t, 0)
+                if n == AHEAD_AT and t == 1:
+                    transpose(n + 2)
+                    quantize(("x",) + divmod(n + 2, 3))
+            nxt = [n + 2] if n < AHEAD_AT else [n + 3]
+            for i in range(GAINS[n]):
+                more_gain()
+            if n in NEAR_AT:
+                near_interleave(NEAR_AT.index(n), 1, N)
+            for m in nxt:
+                if m < UNITS:
+                    transpose(m)
+                    quantize(("x",) + divmod(m, 3))
+            if n in NEAR_AT:
+                quantize(("near", NEAR_AT.index(n), 1))
+            if a == 2:
+                h_interleave(g, 0)
+            for i in range(LOGS[n]):
+                more_log()
+            if a == 0 and g > 0:
+                quantize(("h", g - 1, 0))
+
+        for step in range(ROW_TILES + LEAD):
+            if EARLY <= step < ROW_TILES:
+                blur_right(step)
+            if step >= LEAD:
+                blur_cols(step - LEAD, 0)
+            for i in range(BG[step] if step < len(BG) else 1):
+                more_gain()
+            if step == 0:
+                quantize(("h", GROUPS - 1, 0))
+            if step >= LEAD:
+                log_surround(step - LEAD, 0)
+            if step % 4 == 3 and step < ROW_TILES:
+                h_interleave(step // 4, 1)
+            more_log()
+            if step > LEAD:
+                finish(step - LEAD - 1, 0)
+            if step % 4 == 0 and 0 < step <= ROW_TILES:
+                quantize(("h", step // 4 - 1, 1))
+        for j in range(ROW_TILES):
+            blur_cols(j, 1)
+            more_gain()
+            log_surround(j, 1)
+            more_log()
+            if j == 0:
+                finish(ROW_TILES - 1, 0)
+            else:
+                finish(j - 1, 1)
+        finish(ROW_TILES - 1, 1)
+        assert len(logged) == len(todo)

@@ -26,16 +26,20 @@ ROW_TILES = H // P
 BANKS = 8
 UNITS = 3 * GROUPS
 NEAR_SPLIT = 512
-TURN_BANKS = 3
-GAINS = [0] * 9
-LOGS = [0] * 9
+TURN_BANKS = 2
+GAINS = [1, 1, 1, 0, 0, 1, 0, 1, 1]
+LOGS = [1, 1, 0, 0, 1, 0, 0, 2, 0]
 NEAR_AT = [3, 5]
-LEAD = 5
-AHEAD_AT = 1
+LEAD = 6
+AHEAD_AT = 99
 EARLY = 1
-BG = [0, 0, 0, 2]
+BG = 0
+NARROW = 4
+BPH = 4
+BST = 1
+CPH = 3
 EVAC_V = []
-WARM = [12, 8]
+WARM = [12, 12, 9]
 
 
 def tile_single_scale_retinex_s3_kernel(
@@ -45,7 +49,7 @@ def tile_single_scale_retinex_s3_kernel(
     with ExitStack() as ctx:
         keep = ctx.enter_context(tc.tile_pool(name="keep", bufs=1))
         psum = ctx.enter_context(tc.psum_pool(name="psum", bufs=1))
-        ctx.enter_context(tc.manual_schedule(engines={mybir.EngineType.PE, mybir.EngineType.SP, mybir.EngineType.Pool}))
+        ctx.enter_context(tc.manual_schedule())
 
         def sbuf(name, shape, dtype):
             return keep.tile(shape, dtype, name=name, align_bytes=64)
@@ -67,15 +71,13 @@ def tile_single_scale_retinex_s3_kernel(
 
         near_rows = near.rearrange("(a p j) c -> a p j c", p=P, j=PACK)
         tile_rows = tile.rearrange("(j p) c -> p j c", p=P)
+        out_rows = out.rearrange("(j p) c -> p j c", p=P)
         halo_rows = halo.rearrange("(j p) c -> p j c", p=P)
 
         ident = sbuf("ident", [P, P], F32)
         make_identity(nc, ident[:])
         far_plane = sbuf("far_plane", [P, W], U8)
         down_plane = sbuf("down_plane", [P, GROUPS * H], U8)
-        one = sbuf("one", [P, 1], F32)
-        warm = sbuf("warm", [P, 1], F32)
-        nc.vector.memset(one[:], 1.0)
         zeros = sbuf("zeros", [P, PACK * P], BF16)
         zero_codes = sbuf("zero_codes", [P, P], U32)
         zero_scales = sbuf("zero_scales", [P, P], U8)
@@ -83,20 +85,22 @@ def tile_single_scale_retinex_s3_kernel(
         nc.vector.memset(far_plane[:].bitcast(I32), 0)
         nc.vector.quantize_mx(out=zero_codes[:].bitcast(FP8X4), scales=zero_scales[:], in_=zeros[:])
         nc.gpsimd.memset(down_plane[:].bitcast(I32), 0)
-        nc.scalar.activation(out=warm[:], in_=one[:], func=ACT.Ln)
 
-        rows_in, near_in = {}, {}
+        rows_in, pair_in, near_in = {}, {}, {}
 
-        def load_unit(n, pieces=1):
+        def load_rows(n, first, count):
             g, a = divmod(n, 3)
             src = tile_rows[:, :, cols(a)] if a < 2 else halo_rows
-            per = PACK // pieces
-            for i in range(pieces):
-                j0 = PACK * g + per * i
-                raw = sbuf("rows%d_%d" % (n, i), [P, per, N], BF16)
-                nc.sync.dma_start(out=raw[:], in_=src[:, j0 : j0 + per, :])
-                for j in range(per):
-                    rows_in[j0 + j, a] = raw[:, j, :]
+            j0 = PACK * g + first
+            raw = sbuf("rows%d_%d" % (n, first), [P, count, N], BF16)
+            nc.sync.dma_start(out=raw[:], in_=src[:, j0 : j0 + count, :])
+            for j in range(count):
+                rows_in[j0 + j, a] = raw[:, j, :]
+            for j in range(0, count, 2):
+                pair_in[(j0 + j) // 2, a] = raw[:, j : j + 2, :]
+
+        def load_unit(n):
+            load_rows(n, 0, PACK)
 
         def load_near(a, half):
             raw = sbuf("near%d_%d" % (a, half), [P, PACK, N], BF16)
@@ -111,9 +115,12 @@ def tile_single_scale_retinex_s3_kernel(
         gain_col = sbuf("gain_col", [P, 8], F32)
         gain = sbuf("gain", [P, W], F32)
 
-        nc.sync.dma_start(out=gain_raw[:], in_=col_gain.rearrange("(n m) -> n m", m=8))
+        nc.sync.dma_start(
+            out=gain_raw[:].rearrange("n (b m) -> n b m", b=2), in_=col_gain.rearrange("(b n m) -> n b m", b=2, m=4)
+        )
+        load_rows(0, 0, 2)
         load_near(0, 0)
-        load_unit(0)
+        load_rows(0, 2, 2)
         load_unit(1)
         for q in range(4):
             nc.sync.dma_start(
@@ -122,9 +129,10 @@ def tile_single_scale_retinex_s3_kernel(
         load_near(1, 0)
         load_unit(2)
         nc.sync.dma_start(out=far[:].bitcast(I32), in_=far_words[0].bitcast(I32))
-        nc.sync.dma_start(out=weight_raw[:], in_=row_weight.rearrange("(g p t) -> p g t", p=P, t=PACK))
         for n in range(3, UNITS):
             load_unit(n)
+            if n == 3:
+                nc.sync.dma_start(out=weight_raw[:], in_=row_weight.rearrange("(g p t) -> p g t", p=P, t=PACK))
             if n in (5, 6):
                 load_near(n - 5, 1)
         nc.sync.dma_start(
@@ -137,7 +145,7 @@ def tile_single_scale_retinex_s3_kernel(
                 in_=down_scales.bitcast(I32)[:, 4 * q : 4 * q + 4, :].rearrange("g r n -> r g n"),
             )
 
-        grouped, mx, turned, sums, rounded, logs, lsur = {}, {}, {}, {}, {}, {}, {}
+        grouped, mx, spread, sums, rounded, logs, lsur = {}, {}, {}, {}, {}, {}, {}
 
         def interleave(engine_copy, key, src, c0, c1):
             engine_copy(
@@ -161,13 +169,14 @@ def tile_single_scale_retinex_s3_kernel(
             if split < N:
                 interleave(nc.scalar.copy, key, near_in[a, half], split, N)
 
-        def transpose(n):
+        def transpose(n, halves=(0, 1)):
             g, a = divmod(n, 3)
             key = ("x", g, a)
-            grouped[key] = ring(keep, "wide", 5, [P, N, PACK], BF16)
+            if halves[0] == 0:
+                grouped[key] = ring(keep, "wide", 5, [P, N, PACK], BF16)
             dst = grouped[key][:].rearrange("p c t -> p (c t)").bitcast(F32)
             dst = dst.rearrange("p (t j m u) -> p j t m u", t=PACK, j=PACK, u=2)
-            for b in range(2):
+            for b in halves:
                 ps = bank("turn", 0, TURN_BANKS)
                 for i in range(2):
                     words = rows_in[PACK * g + 2 * b + i, a].bitcast(F32)
@@ -190,16 +199,18 @@ def tile_single_scale_retinex_s3_kernel(
                     stop=True,
                 )
 
-        def spread_gain():
-            for b in range(2):
-                ps = bank("turn", 0, TURN_BANKS)
-                for m in range(4):
-                    src = gain_col[:, 4 * b + m : 4 * b + m + 1].to_broadcast([P, P])
-                    nc.tensor.transpose(ps[:, m * P : (m + 1) * P], src, ident[:])
-                nc.vector.tensor_copy(
-                    out=gain[:].rearrange("p (n m) -> p n m", m=8)[:, :, 4 * b : 4 * b + 4],
-                    in_=ps[:].rearrange("p (m n) -> p n m", m=4),
-                )
+        def spread_gain(b):
+            ps = psum.tile([P, N], F32, name="bank6")
+            for m in range(4):
+                src = gain_col[:, 4 * b + m : 4 * b + m + 1].to_broadcast([P, P])
+                nc.tensor.transpose(ps[:, m * P : (m + 1) * P], src, ident[:])
+            spread[b] = ps
+
+        def empty_gain(b):
+            nc.vector.tensor_copy(
+                out=gain[:, cols(b)].rearrange("p (n m) -> p n m", m=4),
+                in_=spread[b][:].rearrange("p (m n) -> p n m", m=4),
+            )
 
         def blur_pass(g, t, half, a):
             if a == 0:
@@ -246,111 +257,131 @@ def tile_single_scale_retinex_s3_kernel(
                 )
             sums["s", j, half] = ps
 
-        def gain_tile(j, half):
-            logs[j, half] = sbuf("log%d_%d" % (j, half), [P, N], F32)
-            nc.vector.tensor_tensor(out=logs[j, half][:], in0=rows_in[j, half], in1=gain[:, cols(half)], op=ALU.mult)
+        def log_tile(i, half):
+            logs[i, half] = sbuf("log%d_%d" % (i, half), [P, 2, N], F32)
+            nc.scalar.activation(out=logs[i, half][:], in_=pair_in[i, half], func=ACT.Ln)
 
-        def log_tile(j, half):
-            nc.scalar.activation(out=logs[j, half][:], in_=logs[j, half][:], func=ACT.Ln)
+        def gain_tile(i, half):
+            nc.vector.tensor_tensor(
+                out=logs[i, half][:],
+                in0=logs[i, half][:],
+                in1=gain[:, cols(half)].unsqueeze(1).to_broadcast([P, 2, N]),
+                op=ALU.add,
+            )
 
-        def log_surround(j, half):
-            lsur[j, half] = ring(keep, "lsur", 4, [P, N], F32)
-            nc.scalar.activation(out=lsur[j, half][:], in_=sums["s", j, half][:], func=ACT.Ln)
+        def log_surround(j, half, c0=0, c1=N):
+            if j % 2 == 0 and c0 == 0:
+                lsur[j // 2, half] = ring(keep, "lsur", 3, [P, 2, N], F32)
+            nc.scalar.activation(out=lsur[j // 2, half][:, j % 2, c0:c1], in_=sums["s", j, half][:, c0:c1], func=ACT.Ln)
 
-        def finish(j, half):
-            nc.vector.tensor_tensor(out=logs[j, half][:], in0=logs[j, half][:], in1=lsur[j, half][:], op=ALU.subtract)
-            nc.sync.dma_start(out=out[j * P : (j + 1) * P, cols(half)], in_=logs[j, half][:])
+        def finish(j0, count, half, c0=0, c1=N):
+            part = logs[j0 // 2, half][:, j0 % 2 : j0 % 2 + count, c0:c1]
+            sub = lsur[j0 // 2, half][:, j0 % 2 : j0 % 2 + count, c0:c1]
+            nc.vector.tensor_tensor(out=part, in0=part, in1=sub, op=ALU.subtract)
+            nc.sync.dma_start(out=out_rows[:, j0 : j0 + count, half * N + c0 : half * N + c1], in_=part)
 
-        todo = [(j, half) for half in range(2) for j in range(ROW_TILES)]
+        todo = [(2 * g + i, half) for g in range(GROUPS) for half in range(2) for i in range(2)]
         gained, logged = [], []
 
         def more_gain():
-            if len(gained) < len(todo):
+            if len(gained) < len(logged):
                 gain_tile(*todo[len(gained)])
                 gained.append(1)
 
         def more_log():
-            if len(logged) < len(gained):
+            if len(logged) < len(todo):
                 log_tile(*todo[len(logged)])
                 logged.append(1)
 
         keep_warm(WARM[0])
-        nc.vector.tensor_copy(out=gain_col[:], in_=gain_raw[:])
-        spread_gain()
+        nc.scalar.activation(out=gain_col[:], in_=gain_raw[:], func=ACT.Ln)
+        transpose(0, (0,))
         keep_warm(WARM[1])
-        transpose(0)
-        keep_warm(WARM[1])
+        more_log()
         near_interleave(0, 0, NEAR_SPLIT)
-        quantize(("x", 0, 0))
+        spread_gain(0)
+        transpose(0, (1,))
+        keep_warm(WARM[2])
+        more_log()
+        empty_gain(0)
         quantize(("near", 0, 0))
-        transpose(1)
-        more_gain()
+        quantize(("x", 0, 0))
         near_interleave(1, 0, NEAR_SPLIT)
-        quantize(("x", 0, 1))
-        nc.vector.tensor_copy(out=weight[:], in_=weight_raw[:])
-        quantize(("near", 1, 0))
 
         def blur_right(step):
             for a in range(3):
                 blur_pass(*divmod(step, PACK), 1, a)
-            empty_sums(*divmod(step, PACK), 1)
 
         for n in range(UNITS):
             g, a = divmod(n, 3)
+            if n == 1:
+                spread_gain(1)
+            if n + 1 < UNITS:
+                transpose(n + 1)
+                quantize(("x",) + divmod(n + 1, 3))
+            if n == 0:
+                quantize(("near", 1, 0))
+            if g > 0 and a == 2:
+                quantize(("h", g - 1, 0))
+            if n == 1:
+                empty_gain(1)
+                nc.vector.tensor_copy(out=weight[:], in_=weight_raw[:])
             if n == UNITS - 1:
-                for step in range(EARLY):
-                    blur_right(step)
+                blur_right(0)
             for t in range(PACK):
                 blur_pass(g, t, 0, a)
-                if a == 2:
-                    empty_sums(g, t, 0)
-                if n == AHEAD_AT and t == 1:
-                    transpose(n + 2)
-                    quantize(("x",) + divmod(n + 2, 3))
-            nxt = [n + 2] if n < AHEAD_AT else [n + 3]
-            for i in range(GAINS[n]):
-                more_gain()
-            if n in NEAR_AT:
-                near_interleave(NEAR_AT.index(n), 1, N)
-            for m in nxt:
-                if m < UNITS:
-                    transpose(m)
-                    quantize(("x",) + divmod(m, 3))
-            if n in NEAR_AT:
-                quantize(("near", NEAR_AT.index(n), 1))
-            if a == 2:
-                h_interleave(g, 0)
             for i in range(LOGS[n]):
                 more_log()
-            if a == 0 and g > 0:
-                quantize(("h", g - 1, 0))
-
-        for step in range(ROW_TILES + LEAD):
-            if EARLY <= step < ROW_TILES:
-                blur_right(step)
-            if step >= LEAD:
-                blur_cols(step - LEAD, 0)
-            for i in range(BG[step] if step < len(BG) else 1):
+            if a == 2:
+                empty_sums(g, 0, 0)
+                empty_sums(g, 1, 0)
+            if g > 0 and a == 0:
+                empty_sums(g - 1, 2, 0)
+                empty_sums(g - 1, 3, 0)
+                near_interleave(g - 1, 1, N)
+                quantize(("near", g - 1, 1))
+            if g > 0 and a == 1:
+                h_interleave(g - 1, 0)
+            for i in range(GAINS[n]):
                 more_gain()
-            if step == 0:
-                quantize(("h", GROUPS - 1, 0))
-            if step >= LEAD:
-                log_surround(step - LEAD, 0)
+        empty_sums(GROUPS - 1, 2, 0)
+        empty_sums(GROUPS - 1, 3, 0)
+        h_interleave(GROUPS - 1, 0)
+        empty_sums(0, 0, 1)
+        more_gain()
+        quantize(("h", GROUPS - 1, 0))
+
+        for step in range(1, ROW_TILES + LEAD):
+            j = step - LEAD
+            if step < ROW_TILES:
+                blur_right(step)
+                empty_sums(*divmod(step, PACK), 1)
+            if j >= 0:
+                blur_cols(j, 0)
+                log_surround(j, 0)
+            if step % BPH == BST:
+                more_log()
             if step % 4 == 3 and step < ROW_TILES:
                 h_interleave(step // 4, 1)
-            more_log()
-            if step > LEAD:
-                finish(step - LEAD - 1, 0)
-            if step % 4 == 0 and 0 < step <= ROW_TILES:
-                quantize(("h", step // 4 - 1, 1))
+            if j >= 0 and j % 2 == 1:
+                finish(j - 1, 2, 0)
+            else:
+                more_gain()
+            if step % 4 == 3 and step < ROW_TILES:
+                quantize(("h", step // 4, 1))
         for j in range(ROW_TILES):
             blur_cols(j, 1)
-            more_gain()
-            log_surround(j, 1)
-            more_log()
-            if j == 0:
-                finish(ROW_TILES - 1, 0)
+            if j < ROW_TILES - 1:
+                log_surround(j, 1)
+                if j % CPH == 0:
+                    more_log()
+                more_gain()
+                if j >= ROW_TILES - NARROW:
+                    finish(j, 1, 1)
+                elif j % 2 == 1:
+                    finish(j - 1, 2, 1)
             else:
-                finish(j - 1, 1)
-        finish(ROW_TILES - 1, 1)
-        assert len(logged) == len(todo)
+                for c0 in range(0, N, N // 2):
+                    log_surround(j, 1, c0, c0 + N // 2)
+                    finish(j, 1, 1, c0, c0 + N // 2)
+        assert len(gained) == len(todo)

@@ -18,28 +18,20 @@ ALU = mybir.AluOpType
 
 P = 128
 PACK = 4
-K_PASS = P * PACK
 N = 512
-GROUPS = H // K_PASS
-PAIRS = 2 * GROUPS
+GROUPS = H // (P * PACK)
+PASSES = 3
+UNITS = PASSES * GROUPS
 ROW_TILES = H // P
+PAIRS = ROW_TILES // 2
 BANKS = 8
-UNITS = 3 * GROUPS
-NEAR_SPLIT = 512
 TURN_BANKS = 2
-GAINS = [1, 1, 1, 0, 0, 1, 0, 1, 1]
-LOGS = [1, 1, 0, 0, 1, 0, 0, 2, 0]
-NEAR_AT = [3, 5]
-LEAD = 6
-AHEAD_AT = 99
-EARLY = 1
-BG = 0
-NARROW = 4
-BPH = 4
-BST = 1
-CPH = 3
-EVAC_V = []
-WARM = [12, 12, 9]
+STAGED = 5
+ROUNDED = 3
+SURROUND_LOGS = 3
+WARM_PASSES = 9
+LAG = 2
+NARROW = 2
 
 
 def tile_single_scale_retinex_s3_kernel(
@@ -54,30 +46,32 @@ def tile_single_scale_retinex_s3_kernel(
         def sbuf(name, shape, dtype):
             return keep.tile(shape, dtype, name=name, align_bytes=64)
 
-        rings = {}
+        def psum_bank(number):
+            return psum.tile([P, N], F32, name="bank%d" % number)
 
-        def ring(pool, name, depth, shape, dtype):
-            made = rings.setdefault(name, [])
-            made.append(pool.tile(shape, dtype, name="%s%d" % (name, len(made) % depth), align_bytes=64))
-            return made[-1]
+        turns = {}
 
-        def bank(role, first, count):
-            made = rings.setdefault(role, [])
-            made.append(psum.tile([P, N], F32, name="bank%d" % (first + len(made) % count)))
-            return made[-1]
+        def turn(name, depth):
+            calls = turns.setdefault(name, [])
+            calls.append(name)
+            return (len(calls) - 1) % depth
 
         def cols(half):
             return slice(half * N, (half + 1) * N)
 
-        near_rows = near.rearrange("(a p j) c -> a p j c", p=P, j=PACK)
+        near_rows = near.rearrange("(a p t) c -> a p t c", p=P, t=PACK)
         tile_rows = tile.rearrange("(j p) c -> p j c", p=P)
-        out_rows = out.rearrange("(j p) c -> p j c", p=P)
         halo_rows = halo.rearrange("(j p) c -> p j c", p=P)
+        out_rows = out.rearrange("(j p) c -> p j c", p=P)
 
         ident = sbuf("ident", [P, P], F32)
         make_identity(nc, ident[:])
         far_plane = sbuf("far_plane", [P, W], U8)
         down_plane = sbuf("down_plane", [P, GROUPS * H], U8)
+        one = sbuf("one", [P, 1], F32)
+        log_one = sbuf("log_one", [P, 1], F32)
+        nc.vector.memset(one[:], 1.0)
+        nc.scalar.activation(out=log_one[:], in_=one[:], func=ACT.Ln)
         zeros = sbuf("zeros", [P, PACK * P], BF16)
         zero_codes = sbuf("zero_codes", [P, P], U32)
         zero_scales = sbuf("zero_scales", [P, P], U8)
@@ -86,111 +80,100 @@ def tile_single_scale_retinex_s3_kernel(
         nc.vector.quantize_mx(out=zero_codes[:].bitcast(FP8X4), scales=zero_scales[:], in_=zeros[:])
         nc.gpsimd.memset(down_plane[:].bitcast(I32), 0)
 
-        rows_in, pair_in, near_in = {}, {}, {}
+        pair_rows, near_raw = {}, {}
 
-        def load_rows(n, first, count):
-            g, a = divmod(n, 3)
-            src = tile_rows[:, :, cols(a)] if a < 2 else halo_rows
-            j0 = PACK * g + first
-            raw = sbuf("rows%d_%d" % (n, first), [P, count, N], BF16)
-            nc.sync.dma_start(out=raw[:], in_=src[:, j0 : j0 + count, :])
-            for j in range(count):
-                rows_in[j0 + j, a] = raw[:, j, :]
-            for j in range(0, count, 2):
-                pair_in[(j0 + j) // 2, a] = raw[:, j : j + 2, :]
-
-        def load_unit(n):
-            load_rows(n, 0, PACK)
+        def load_rows(n, first_pair, pairs):
+            g, a = divmod(n, PASSES)
+            source = tile_rows[:, :, cols(a)] if a < 2 else halo_rows
+            j0 = PACK * g + 2 * first_pair
+            raw = sbuf("rows%d_%d" % (n, first_pair), [P, 2 * pairs, N], BF16)
+            nc.sync.dma_start(out=raw[:], in_=source[:, j0 : j0 + 2 * pairs, :])
+            for i in range(pairs):
+                pair_rows[j0 // 2 + i, a] = raw[:, 2 * i : 2 * i + 2, :]
 
         def load_near(a, half):
-            raw = sbuf("near%d_%d" % (a, half), [P, PACK, N], BF16)
-            nc.sync.dma_start(out=raw[:], in_=near_rows[a][:, :, cols(half)])
-            near_in[a, half] = raw
+            near_raw[a, half] = sbuf("near%d_%d" % (a, half), [P, PACK, N], BF16)
+            nc.sync.dma_start(out=near_raw[a, half][:], in_=near_rows[a][:, :, cols(half)])
+
+        def load_scales(plane, scales):
+            passes = scales.shape[0]
+            for q in range(4):
+                nc.sync.dma_start(
+                    out=plane[32 * q : 32 * q + 4, :].bitcast(I32).rearrange("r (g n) -> r g n", g=passes),
+                    in_=scales.bitcast(I32)[:, 4 * q : 4 * q + 4, :].rearrange("g r n -> r g n"),
+                )
 
         far = sbuf("far", [P, 2 * W], U8)
         down = sbuf("down", [P, GROUPS * 2 * H], U8)
         weight_raw = sbuf("weight_raw", [P, GROUPS, PACK], BF16)
         weight = sbuf("weight", [P, GROUPS, PACK], F32)
-        gain_raw = sbuf("gain_raw", [P, 8], BF16)
-        gain_col = sbuf("gain_col", [P, 8], F32)
-        gain = sbuf("gain", [P, W], F32)
+        gain_raw = sbuf("gain_raw", [P, 2, PACK], BF16)
+        log_gain_col = sbuf("log_gain_col", [P, 2, PACK], F32)
+        log_gain = sbuf("log_gain", [P, W], F32)
 
-        nc.sync.dma_start(
-            out=gain_raw[:].rearrange("n (b m) -> n b m", b=2), in_=col_gain.rearrange("(b n m) -> n b m", b=2, m=4)
-        )
-        load_rows(0, 0, 2)
+        nc.sync.dma_start(out=gain_raw[:], in_=col_gain.rearrange("(b p m) -> p b m", b=2, m=PACK))
+        load_rows(0, 0, 1)
         load_near(0, 0)
-        load_rows(0, 2, 2)
-        load_unit(1)
-        for q in range(4):
-            nc.sync.dma_start(
-                out=far_plane[32 * q : 32 * q + 4, :].bitcast(I32), in_=far_scales[0][4 * q : 4 * q + 4, :].bitcast(I32)
-            )
+        load_rows(0, 1, 1)
+        load_rows(1, 0, 2)
+        load_scales(far_plane, far_scales)
         load_near(1, 0)
-        load_unit(2)
+        load_rows(2, 0, 2)
         nc.sync.dma_start(out=far[:].bitcast(I32), in_=far_words[0].bitcast(I32))
-        for n in range(3, UNITS):
-            load_unit(n)
-            if n == 3:
-                nc.sync.dma_start(out=weight_raw[:], in_=row_weight.rearrange("(g p t) -> p g t", p=P, t=PACK))
-            if n in (5, 6):
-                load_near(n - 5, 1)
+        load_rows(3, 0, 2)
+        nc.sync.dma_start(out=weight_raw[:], in_=row_weight.rearrange("(g p t) -> p g t", p=P, t=PACK))
+        load_rows(4, 0, 2)
+        for a in range(2):
+            load_rows(5 + a, 0, 2)
+            load_near(a, 1)
+        load_rows(7, 0, 2)
+        load_rows(8, 0, 2)
         nc.sync.dma_start(
             out=down[:].bitcast(I32).rearrange("p (g n) -> p g n", g=GROUPS),
             in_=down_words.bitcast(I32).rearrange("g p n -> p g n"),
         )
-        for q in range(4):
-            nc.sync.dma_start(
-                out=down_plane[32 * q : 32 * q + 4, :].bitcast(I32).rearrange("r (g n) -> r g n", g=GROUPS),
-                in_=down_scales.bitcast(I32)[:, 4 * q : 4 * q + 4, :].rearrange("g r n -> r g n"),
-            )
+        load_scales(down_plane, down_scales)
 
-        grouped, mx, spread, sums, rounded, logs, lsur = {}, {}, {}, {}, {}, {}, {}
+        staged, quantised, sums, rounded, result, log_sur = {}, {}, {}, {}, {}, {}
 
-        def interleave(engine_copy, key, src, c0, c1):
-            engine_copy(
-                out=grouped[key][:, c0:c1, :].rearrange("p (c i) t -> p c t i", i=4),
-                in_=src[:, :, c0:c1].rearrange("p t (c i) -> p c t i", i=4),
+        def stage(key):
+            staged[key] = sbuf("staged%d" % turn("staged", STAGED), [P, N, PACK], BF16)
+            return staged[key]
+
+        def interleave(key, source):
+            nc.vector.tensor_copy(
+                out=stage(key)[:].rearrange("p (c i) t -> p c t i", i=4),
+                in_=source[:].rearrange("p t (c i) -> p c t i", i=4),
             )
 
         def quantize(key):
-            src = grouped[key]
-            width = src.shape[1]
-            name = "_".join([str(x) for x in key])
-            codes = sbuf("codes" + name, [P, width], U32)
-            scales = sbuf("scales" + name, [P, width], U8)
-            nc.vector.quantize_mx(out=codes[:].bitcast(FP8X4), scales=scales[:], in_=src[:].rearrange("p c t -> p (c t)"))
-            mx[key] = (codes, scales)
+            name = "%s%d_%d" % key
+            codes = sbuf("codes_" + name, [P, N], U32)
+            scales = sbuf("scales_" + name, [P, N], U8)
+            nc.vector.quantize_mx(
+                out=codes[:].bitcast(FP8X4), scales=scales[:], in_=staged[key][:].rearrange("p c t -> p (c t)")
+            )
+            quantised[key] = (codes, scales)
 
-        def near_interleave(a, half, split):
-            key = ("near", a, half)
-            grouped[key] = ring(keep, "wide", 5, [P, N, PACK], BF16)
-            interleave(nc.vector.tensor_copy, key, near_in[a, half], 0, split)
-            if split < N:
-                interleave(nc.scalar.copy, key, near_in[a, half], split, N)
+        def transpose_pair(n, i):
+            g, a = divmod(n, PASSES)
+            target = stage(("rows", g, a)) if i == 0 else staged["rows", g, a]
+            target = target[:].rearrange("p c t -> p (c t)").bitcast(F32)
+            target = target.rearrange("p (t j m u) -> p j t m u", t=PACK, j=PACK, u=2)
+            bank = psum_bank(turn("turn", TURN_BANKS))
+            for j in range(2):
+                words = pair_rows[2 * g + i, a][:, j, :].bitcast(F32)
+                for u in range(2):
+                    nc.tensor.transpose(bank[:, (2 * j + u) * P : (2 * j + u + 1) * P], words[:, u : 2 * P : 2], ident[:])
+            nc.scalar.copy(
+                out=target[:, 2 * i : 2 * i + 2], in_=bank[:].rearrange("p (j u m t) -> p j t m u", j=2, u=2, t=PACK)
+            )
 
-        def transpose(n, halves=(0, 1)):
-            g, a = divmod(n, 3)
-            key = ("x", g, a)
-            if halves[0] == 0:
-                grouped[key] = ring(keep, "wide", 5, [P, N, PACK], BF16)
-            dst = grouped[key][:].rearrange("p c t -> p (c t)").bitcast(F32)
-            dst = dst.rearrange("p (t j m u) -> p j t m u", t=PACK, j=PACK, u=2)
-            for b in halves:
-                ps = bank("turn", 0, TURN_BANKS)
-                for i in range(2):
-                    words = rows_in[PACK * g + 2 * b + i, a].bitcast(F32)
-                    for u in range(2):
-                        nc.tensor.transpose(ps[:, (2 * i + u) * P : (2 * i + u + 1) * P], words[:, u : 2 * P : 2], ident[:])
-                (nc.vector.tensor_copy if 2 * n + b in EVAC_V else nc.scalar.copy)(
-                    out=dst[:, 2 * b : 2 * b + 2], in_=ps[:].rearrange("p (j u m t) -> p j t m u", j=2, u=2, t=PACK)
-                )
-
-        def keep_warm(count):
-            ps = psum.tile([P, N], F32, name="bank7")
-            for i in range(count):
+        def keep_warm():
+            bank = psum_bank(BANKS - 1)
+            for i in range(WARM_PASSES):
                 nc.tensor.matmul_mx(
-                    out=ps[:, (i % 4) * P : (i % 4 + 1) * P],
+                    out=bank[:, (i % 4) * P : (i % 4 + 1) * P],
                     lhsT=zero_codes[:].bitcast(FP8X4),
                     lhsT_scale=zero_scales[:],
                     rhs=zero_codes[:].bitcast(FP8X4),
@@ -199,25 +182,24 @@ def tile_single_scale_retinex_s3_kernel(
                     stop=True,
                 )
 
-        def spread_gain(b):
-            ps = psum.tile([P, N], F32, name="bank6")
-            for m in range(4):
-                src = gain_col[:, 4 * b + m : 4 * b + m + 1].to_broadcast([P, P])
-                nc.tensor.transpose(ps[:, m * P : (m + 1) * P], src, ident[:])
-            spread[b] = ps
-
-        def empty_gain(b):
+        def spread_log_gain(half):
+            bank = psum_bank(TURN_BANKS + half)
+            for m in range(PACK):
+                column = log_gain_col[:, half, m : m + 1].to_broadcast([P, P])
+                nc.tensor.transpose(bank[:, m * P : (m + 1) * P], column, ident[:])
             nc.vector.tensor_copy(
-                out=gain[:, cols(b)].rearrange("p (n m) -> p n m", m=4),
-                in_=spread[b][:].rearrange("p (m n) -> p n m", m=4),
+                out=log_gain[:, cols(half)].rearrange("p (n m) -> p n m", m=PACK),
+                in_=bank[:].rearrange("p (m n) -> p n m", m=PACK),
             )
 
-        def blur_pass(g, t, half, a):
-            if a == 0:
-                sums[g, t, half] = bank("late", 0, BANKS) if half else bank("sum", TURN_BANKS, BANKS - TURN_BANKS)
-            codes, scales = mx["x", g, a]
+        def row_pass(g, t, half, a):
+            if a == 0 and half == 0:
+                sums[g, t, half] = psum_bank(TURN_BANKS + turn("left", BANKS - TURN_BANKS))
+            elif a == 0:
+                sums[g, t, half] = psum_bank(turn("late", BANKS))
+            codes, scales = quantised["rows", g, a]
             if a < 2:
-                rhs, rhs_scale = mx["near", a, half][0][:].bitcast(FP8X4), mx["near", a, half][1][:]
+                rhs, rhs_scale = quantised["near", a, half][0][:].bitcast(FP8X4), quantised["near", a, half][1][:]
             else:
                 rhs, rhs_scale = far[:, 2 * N * half : 2 * N * (half + 1)].bitcast(FP4X4), far_plane[:, cols(half)]
             nc.tensor.matmul_mx(
@@ -227,161 +209,139 @@ def tile_single_scale_retinex_s3_kernel(
                 rhs=rhs,
                 rhs_scale=rhs_scale,
                 start=(a == 0),
-                stop=(a == 2),
+                stop=(a == PASSES - 1),
             )
 
         def empty_sums(g, t, half):
             if t == 0:
-                rounded[g, half] = ring(keep, "rounded", 3, [P, PACK, N], BF16)
+                rounded[g, half] = sbuf("rounded%d" % turn("rounded", ROUNDED), [P, PACK, N], BF16)
             nc.scalar.activation(
                 out=rounded[g, half][:, t, :], in_=sums[g, t, half][:], func=ACT.Copy, scale=weight[:, g, t : t + 1]
             )
 
-        def h_interleave(g, half):
-            key = ("h", g, half)
-            grouped[key] = ring(keep, "wide", 5, [P, N, PACK], BF16)
-            interleave(nc.vector.tensor_copy, key, rounded[g, half], 0, N)
-
-        def blur_cols(j, half):
-            ps = bank("late", 0, BANKS)
+        def column_blur(j, half):
+            bank = psum_bank(turn("late", BANKS))
             for g in range(GROUPS):
-                codes, scales = mx["h", g, half]
+                codes, scales = quantised["h", g, half]
+                first = g * H + j * P
                 nc.tensor.matmul_mx(
-                    out=ps[:],
-                    lhsT=down[:, 2 * (g * H + j * P) : 2 * (g * H + (j + 1) * P)].bitcast(FP4X4),
-                    lhsT_scale=down_plane[:, g * H + j * P : g * H + (j + 1) * P],
+                    out=bank[:],
+                    lhsT=down[:, 2 * first : 2 * (first + P)].bitcast(FP4X4),
+                    lhsT_scale=down_plane[:, first : first + P],
                     rhs=codes[:].bitcast(FP8X4),
                     rhs_scale=scales[:],
                     start=(g == 0),
                     stop=(g == GROUPS - 1),
                 )
-            sums["s", j, half] = ps
+            return bank
 
-        def log_tile(i, half):
-            logs[i, half] = sbuf("log%d_%d" % (i, half), [P, 2, N], F32)
-            nc.scalar.activation(out=logs[i, half][:], in_=pair_in[i, half], func=ACT.Ln)
+        to_log = [(i, half) for half in range(2) for i in range(2)]
+        to_log.extend([(i, half) for half in range(2) for i in range(2, PAIRS)])
+        to_gain = list(to_log)
 
-        def gain_tile(i, half):
+        def next_log():
+            i, half = to_log[0]
+            to_log.remove((i, half))
+            result[i, half] = sbuf("result%d_%d" % (i, half), [P, 2, N], F32)
+            nc.scalar.activation(out=result[i, half][:], in_=pair_rows[i, half], func=ACT.Ln)
+
+        def next_gain():
+            i, half = to_gain[0]
+            to_gain.remove((i, half))
             nc.vector.tensor_tensor(
-                out=logs[i, half][:],
-                in0=logs[i, half][:],
-                in1=gain[:, cols(half)].unsqueeze(1).to_broadcast([P, 2, N]),
+                out=result[i, half][:],
+                in0=result[i, half][:],
+                in1=log_gain[:, cols(half)].unsqueeze(1).to_broadcast([P, 2, N]),
                 op=ALU.add,
             )
 
-        def log_surround(j, half, c0=0, c1=N):
-            if j % 2 == 0 and c0 == 0:
-                lsur[j // 2, half] = ring(keep, "lsur", 3, [P, 2, N], F32)
-            nc.scalar.activation(out=lsur[j // 2, half][:, j % 2, c0:c1], in_=sums["s", j, half][:, c0:c1], func=ACT.Ln)
+        def finish(i, half, tiles, columns):
+            part = result[i, half][:, tiles, columns]
+            nc.vector.tensor_tensor(out=part, in0=part, in1=log_sur[i, half][:, tiles, columns], op=ALU.subtract)
+            nc.sync.dma_start(out=out_rows[:, 2 * i : 2 * i + 2, cols(half)][:, tiles, columns], in_=part)
 
-        def finish(j0, count, half, c0=0, c1=N):
-            part = logs[j0 // 2, half][:, j0 % 2 : j0 % 2 + count, c0:c1]
-            sub = lsur[j0 // 2, half][:, j0 % 2 : j0 % 2 + count, c0:c1]
-            nc.vector.tensor_tensor(out=part, in0=part, in1=sub, op=ALU.subtract)
-            nc.sync.dma_start(out=out_rows[:, j0 : j0 + count, half * N + c0 : half * N + c1], in_=part)
-
-        todo = [(2 * g + i, half) for g in range(GROUPS) for half in range(2) for i in range(2)]
-        gained, logged = [], []
-
-        def more_gain():
-            if len(gained) < len(logged):
-                gain_tile(*todo[len(gained)])
-                gained.append(1)
-
-        def more_log():
-            if len(logged) < len(todo):
-                log_tile(*todo[len(logged)])
-                logged.append(1)
-
-        keep_warm(WARM[0])
-        nc.scalar.activation(out=gain_col[:], in_=gain_raw[:], func=ACT.Ln)
-        transpose(0, (0,))
-        keep_warm(WARM[1])
-        more_log()
-        near_interleave(0, 0, NEAR_SPLIT)
-        spread_gain(0)
-        transpose(0, (1,))
-        keep_warm(WARM[2])
-        more_log()
-        empty_gain(0)
+        keep_warm()
+        nc.scalar.activation(out=log_gain_col[:], in_=gain_raw[:], func=ACT.Ln)
+        spread_log_gain(0)
+        spread_log_gain(1)
+        next_log()
+        transpose_pair(0, 0)
+        keep_warm()
+        next_log()
+        interleave(("near", 0, 0), near_raw[0, 0])
+        transpose_pair(0, 1)
+        keep_warm()
+        next_log()
         quantize(("near", 0, 0))
-        quantize(("x", 0, 0))
-        near_interleave(1, 0, NEAR_SPLIT)
-
-        def blur_right(step):
-            for a in range(3):
-                blur_pass(*divmod(step, PACK), 1, a)
+        quantize(("rows", 0, 0))
+        interleave(("near", 1, 0), near_raw[1, 0])
+        waiting = [("near", 1, 0)]
 
         for n in range(UNITS):
-            g, a = divmod(n, 3)
-            if n == 1:
-                spread_gain(1)
+            g, a = divmod(n, PASSES)
             if n + 1 < UNITS:
-                transpose(n + 1)
-                quantize(("x",) + divmod(n + 1, 3))
-            if n == 0:
-                quantize(("near", 1, 0))
-            if g > 0 and a == 2:
-                quantize(("h", g - 1, 0))
+                transpose_pair(n + 1, 0)
+                transpose_pair(n + 1, 1)
+                quantize(("rows",) + divmod(n + 1, PASSES))
+            for key in waiting:
+                quantize(key)
+            waiting.clear()
             if n == 1:
-                empty_gain(1)
                 nc.vector.tensor_copy(out=weight[:], in_=weight_raw[:])
-            if n == UNITS - 1:
-                blur_right(0)
+            if n + 1 == UNITS:
+                for first_a in range(PASSES):
+                    row_pass(0, 0, 1, first_a)
             for t in range(PACK):
-                blur_pass(g, t, 0, a)
-            for i in range(LOGS[n]):
-                more_log()
+                row_pass(g, t, 0, a)
             if a == 2:
                 empty_sums(g, 0, 0)
                 empty_sums(g, 1, 0)
-            if g > 0 and a == 0:
+            elif a == 0 and g > 0:
                 empty_sums(g - 1, 2, 0)
                 empty_sums(g - 1, 3, 0)
-                near_interleave(g - 1, 1, N)
-                quantize(("near", g - 1, 1))
-            if g > 0 and a == 1:
-                h_interleave(g - 1, 0)
-            for i in range(GAINS[n]):
-                more_gain()
+            else:
+                next_log()
+            if n + 2 == UNITS:
+                next_log()
+            if a == 1 and g > 0:
+                waiting.append(("h", g - 1, 0))
+                interleave(waiting[0], rounded[g - 1, 0])
+            elif g == 1:
+                waiting.append(("near", a // 2, 1))
+                interleave(waiting[0], near_raw[a // 2, 1])
+            if g != 1:
+                next_gain()
         empty_sums(GROUPS - 1, 2, 0)
         empty_sums(GROUPS - 1, 3, 0)
-        h_interleave(GROUPS - 1, 0)
+        interleave(("h", GROUPS - 1, 0), rounded[GROUPS - 1, 0])
         empty_sums(0, 0, 1)
-        more_gain()
         quantize(("h", GROUPS - 1, 0))
 
-        for step in range(1, ROW_TILES + LEAD):
-            j = step - LEAD
-            if step < ROW_TILES:
-                blur_right(step)
-                empty_sums(*divmod(step, PACK), 1)
-            if j >= 0:
-                blur_cols(j, 0)
-                log_surround(j, 0)
-            if step % BPH == BST:
-                more_log()
-            if step % 4 == 3 and step < ROW_TILES:
-                h_interleave(step // 4, 1)
-            if j >= 0 and j % 2 == 1:
-                finish(j - 1, 2, 0)
-            else:
-                more_gain()
-            if step % 4 == 3 and step < ROW_TILES:
-                quantize(("h", step // 4, 1))
-        for j in range(ROW_TILES):
-            blur_cols(j, 1)
-            if j < ROW_TILES - 1:
-                log_surround(j, 1)
-                if j % CPH == 0:
-                    more_log()
-                more_gain()
-                if j >= ROW_TILES - NARROW:
-                    finish(j, 1, 1)
-                elif j % 2 == 1:
-                    finish(j - 1, 2, 1)
-            else:
-                for c0 in range(0, N, N // 2):
-                    log_surround(j, 1, c0, c0 + N // 2)
-                    finish(j, 1, 1, c0, c0 + N // 2)
-        assert len(gained) == len(todo)
+        for g in range(GROUPS):
+            for t in range(1 if g == 0 else 0, PACK):
+                for a in range(PASSES):
+                    row_pass(g, t, 1, a)
+                empty_sums(g, t, 1)
+            interleave(("h", g, 1), rounded[g, 1])
+            if g + 1 < GROUPS:
+                next_gain()
+            quantize(("h", g, 1))
+
+        order = sorted([(i, half) for i in range(PAIRS) for half in range(2)], key=lambda x: (x[0] + LAG * x[1], x[1]))
+        whole = slice(0, N)
+        for place, (i, half) in enumerate(order):
+            log_sur[i, half] = sbuf("log_sur%d" % turn("log_sur", SURROUND_LOGS), [P, 2, N], F32)
+            narrow = place >= len(order) - NARROW
+            for j in range(2):
+                bank = column_blur(2 * i + j, half)
+                very_last = place == len(order) - 1 and j == 1
+                for columns in [slice(0, N // 2), slice(N // 2, N)] if very_last else [whole]:
+                    nc.scalar.activation(out=log_sur[i, half][:, j, columns], in_=bank[:, columns], func=ACT.Ln)
+                    if narrow:
+                        finish(i, half, slice(j, j + 1), columns)
+            if not narrow:
+                finish(i, half, slice(0, 2), whole)
+            if place % 2 == 0 and to_log:
+                next_log()
+            elif to_gain:
+                next_gain()

@@ -30,8 +30,9 @@ STAGED = 5
 ROUNDED = 3
 SURROUND_LOGS = 3
 WARM_PASSES = 9
+SORTED = (4, 5)
 LAG = 2
-NARROW = 2
+NARROW = 3
 
 
 def tile_single_scale_retinex_s3_kernel(
@@ -80,7 +81,7 @@ def tile_single_scale_retinex_s3_kernel(
         nc.vector.quantize_mx(out=zero_codes[:].bitcast(FP8X4), scales=zero_scales[:], in_=zeros[:])
         nc.gpsimd.memset(down_plane[:].bitcast(I32), 0)
 
-        pair_rows, near_raw = {}, {}
+        pair_rows, unit_rows, near_raw, sorted_words = {}, {}, {}, {}
 
         def load_rows(n, first_pair, pairs):
             g, a = divmod(n, PASSES)
@@ -88,6 +89,7 @@ def tile_single_scale_retinex_s3_kernel(
             j0 = PACK * g + 2 * first_pair
             raw = sbuf("rows%d_%d" % (n, first_pair), [P, 2 * pairs, N], BF16)
             nc.sync.dma_start(out=raw[:], in_=source[:, j0 : j0 + 2 * pairs, :])
+            unit_rows[n] = raw
             for i in range(pairs):
                 pair_rows[j0 // 2 + i, a] = raw[:, 2 * i : 2 * i + 2, :]
 
@@ -124,10 +126,9 @@ def tile_single_scale_retinex_s3_kernel(
         nc.sync.dma_start(out=weight_raw[:], in_=row_weight.rearrange("(g p t) -> p g t", p=P, t=PACK))
         load_rows(4, 0, 2)
         for a in range(2):
-            load_rows(5 + a, 0, 2)
+            load_rows(5 + 2 * a, 0, 2)
+            load_rows(6 + 2 * a, 0, 2)
             load_near(a, 1)
-        load_rows(7, 0, 2)
-        load_rows(8, 0, 2)
         nc.sync.dma_start(
             out=down[:].bitcast(I32).rearrange("p (g n) -> p g n", g=GROUPS),
             in_=down_words.bitcast(I32).rearrange("g p n -> p g n"),
@@ -155,6 +156,12 @@ def tile_single_scale_retinex_s3_kernel(
             )
             quantised[key] = (codes, scales)
 
+        def sort_words(n):
+            sorted_words[n] = sbuf("sorted%d" % turn("sorted", 2), [P, PACK, 2, P], F32)
+            nc.vector.tensor_copy(
+                out=sorted_words[n][:], in_=unit_rows[n][:].bitcast(F32).rearrange("p j (w u) -> p j u w", u=2)
+            )
+
         def transpose_pair(n, i):
             g, a = divmod(n, PASSES)
             target = stage(("rows", g, a)) if i == 0 else staged["rows", g, a]
@@ -162,9 +169,12 @@ def tile_single_scale_retinex_s3_kernel(
             target = target.rearrange("p (t j m u) -> p j t m u", t=PACK, j=PACK, u=2)
             bank = psum_bank(turn("turn", TURN_BANKS))
             for j in range(2):
-                words = pair_rows[2 * g + i, a][:, j, :].bitcast(F32)
                 for u in range(2):
-                    nc.tensor.transpose(bank[:, (2 * j + u) * P : (2 * j + u + 1) * P], words[:, u : 2 * P : 2], ident[:])
+                    if n in SORTED:
+                        words = sorted_words[n][:, 2 * i + j, u, :]
+                    else:
+                        words = pair_rows[2 * g + i, a][:, j, :].bitcast(F32)[:, u : 2 * P : 2]
+                    nc.tensor.transpose(bank[:, (2 * j + u) * P : (2 * j + u + 1) * P], words, ident[:])
             nc.scalar.copy(
                 out=target[:, 2 * i : 2 * i + 2], in_=bank[:].rearrange("p (j u m t) -> p j t m u", j=2, u=2, t=PACK)
             )
@@ -282,6 +292,8 @@ def tile_single_scale_retinex_s3_kernel(
             if n + 1 < UNITS:
                 transpose_pair(n + 1, 0)
                 transpose_pair(n + 1, 1)
+                if n + 2 in SORTED:
+                    sort_words(n + 2)
                 quantize(("rows",) + divmod(n + 1, PASSES))
             for key in waiting:
                 quantize(key)
@@ -322,10 +334,15 @@ def tile_single_scale_retinex_s3_kernel(
                 for a in range(PASSES):
                     row_pass(g, t, 1, a)
                 empty_sums(g, t, 1)
+            if g == 1:
+                next_log()
             interleave(("h", g, 1), rounded[g, 1])
             if g + 1 < GROUPS:
                 next_gain()
-            quantize(("h", g, 1))
+                quantize(("h", g, 1))
+            else:
+                quantize(("h", g, 1))
+                next_gain()
 
         order = sorted([(i, half) for i in range(PAIRS) for half in range(2)], key=lambda x: (x[0] + LAG * x[1], x[1]))
         whole = slice(0, N)

@@ -29,7 +29,6 @@ TURN_BANKS = 2
 STAGED = 5
 ROUNDED = 3
 SURROUND_LOGS = 3
-WARM_PASSES = 9
 SORTED = (4, 5)
 LAG = 2
 NARROW = 3
@@ -69,16 +68,7 @@ def tile_single_scale_retinex_s3_kernel(
         make_identity(nc, ident[:])
         far_plane = sbuf("far_plane", [P, W], U8)
         down_plane = sbuf("down_plane", [P, GROUPS * H], U8)
-        one = sbuf("one", [P, 1], F32)
-        log_one = sbuf("log_one", [P, 1], F32)
-        nc.vector.memset(one[:], 1.0)
-        nc.scalar.activation(out=log_one[:], in_=one[:], func=ACT.Ln)
-        zeros = sbuf("zeros", [P, PACK * P], BF16)
-        zero_codes = sbuf("zero_codes", [P, P], U32)
-        zero_scales = sbuf("zero_scales", [P, P], U8)
-        nc.vector.memset(zeros[:], 0.0)
         nc.vector.memset(far_plane[:].bitcast(I32), 0)
-        nc.vector.quantize_mx(out=zero_codes[:].bitcast(FP8X4), scales=zero_scales[:], in_=zeros[:])
         nc.gpsimd.memset(down_plane[:].bitcast(I32), 0)
 
         pair_rows, unit_rows, near_raw, sorted_words = {}, {}, {}, {}
@@ -179,19 +169,6 @@ def tile_single_scale_retinex_s3_kernel(
                 out=target[:, 2 * i : 2 * i + 2], in_=bank[:].rearrange("p (j u m t) -> p j t m u", j=2, u=2, t=PACK)
             )
 
-        def keep_warm():
-            bank = psum_bank(BANKS - 1)
-            for i in range(WARM_PASSES):
-                nc.tensor.matmul_mx(
-                    out=bank[:, (i % 4) * P : (i % 4 + 1) * P],
-                    lhsT=zero_codes[:].bitcast(FP8X4),
-                    lhsT_scale=zero_scales[:],
-                    rhs=zero_codes[:].bitcast(FP8X4),
-                    rhs_scale=zero_scales[:],
-                    start=True,
-                    stop=True,
-                )
-
         def spread_log_gain(half):
             bank = psum_bank(TURN_BANKS + half)
             for m in range(PACK):
@@ -270,17 +247,14 @@ def tile_single_scale_retinex_s3_kernel(
             nc.vector.tensor_tensor(out=part, in0=part, in1=log_sur[i, half][:, tiles, columns], op=ALU.subtract)
             nc.sync.dma_start(out=out_rows[:, 2 * i : 2 * i + 2, cols(half)][:, tiles, columns], in_=part)
 
-        keep_warm()
         nc.scalar.activation(out=log_gain_col[:], in_=gain_raw[:], func=ACT.Ln)
         spread_log_gain(0)
         spread_log_gain(1)
         next_log()
         transpose_pair(0, 0)
-        keep_warm()
         next_log()
         interleave(("near", 0, 0), near_raw[0, 0])
         transpose_pair(0, 1)
-        keep_warm()
         next_log()
         quantize(("near", 0, 0))
         quantize(("rows", 0, 0))

from contextlib import ExitStack

import concourse.mybir as mybir
from concourse.masks import make_identity

H, W, Z = 1536, 1024, 512
FLOPS = 2 * H * W * (W + Z) + 2 * H * H * W

F32 = mybir.dt.float32
BF16 = mybir.dt.bfloat16
I32 = mybir.dt.int32
U32 = mybir.dt.uint32
U8 = mybir.dt.uint8
FP8X4 = mybir.dt.float8_e4m3fn_x4
FP4X4 = mybir.dt.float4_e2m1fn_x4
ACT = mybir.ActivationFunctionType
ALU = mybir.AluOpType

P = 128
PACK = 4
N = 512
GROUPS = H // (P * PACK)
PASSES = 3
UNITS = PASSES * GROUPS
ROW_TILES = H // P
PAIRS = ROW_TILES // 2
BANKS = 8
TURN_BANKS = 2
STAGED = 5
ROUNDED = 3
SURROUND_LOGS = 3
SORTED = (4, 5)
LAG = 2
NARROW = 3


def tile_single_scale_retinex_s3_kernel(
    tc, tile, halo, near, far_words, far_scales, row_weight, down_words, down_scales, col_gain, out
):
    nc = tc.nc
    with ExitStack() as ctx:
        keep = ctx.enter_context(tc.tile_pool(name="keep", bufs=1))
        psum = ctx.enter_context(tc.psum_pool(name="psum", bufs=1))
        ctx.enter_context(tc.manual_schedule())

        def sbuf(name, shape, dtype):
            return keep.tile(shape, dtype, name=name, align_bytes=64)

        def psum_bank(number):
            return psum.tile([P, N], F32, name="bank%d" % number)

        turns = {}

        def turn(name, depth):
            calls = turns.setdefault(name, [])
            calls.append(name)
            return (len(calls) - 1) % depth

        def cols(half):
            return slice(half * N, (half + 1) * N)

        near_rows = near.rearrange("(a p t) c -> a p t c", p=P, t=PACK)
        tile_rows = tile.rearrange("(j p) c -> p j c", p=P)
        halo_rows = halo.rearrange("(j p) c -> p j c", p=P)
        out_rows = out.rearrange("(j p) c -> p j c", p=P)

        ident = sbuf("ident", [P, P], F32)
        make_identity(nc, ident[:])
        far_plane = sbuf("far_plane", [P, W], U8)
        down_plane = sbuf("down_plane", [P, GROUPS * H], U8)
        nc.vector.memset(far_plane[:].bitcast(I32), 0)
        nc.gpsimd.memset(down_plane[:].bitcast(I32), 0)

        pair_rows, unit_rows, near_raw, sorted_words = {}, {}, {}, {}

        def load_rows(n, first_pair, pairs):
            g, a = divmod(n, PASSES)
            source = tile_rows[:, :, cols(a)] if a < 2 else halo_rows
            j0 = PACK * g + 2 * first_pair
            raw = sbuf("rows%d_%d" % (n, first_pair), [P, 2 * pairs, N], BF16)
            nc.sync.dma_start(out=raw[:], in_=source[:, j0 : j0 + 2 * pairs, :])
            unit_rows[n] = raw
            for i in range(pairs):
                pair_rows[j0 // 2 + i, a] = raw[:, 2 * i : 2 * i + 2, :]

        def load_near(a, half):
            near_raw[a, half] = sbuf("near%d_%d" % (a, half), [P, PACK, N], BF16)
            nc.sync.dma_start(out=near_raw[a, half][:], in_=near_rows[a][:, :, cols(half)])

        def load_scales(plane, scales):
            passes = scales.shape[0]
            for q in range(4):
                nc.sync.dma_start(
                    out=plane[32 * q : 32 * q + 4, :].bitcast(I32).rearrange("r (g n) -> r g n", g=passes),
                    in_=scales.bitcast(I32)[:, 4 * q : 4 * q + 4, :].rearrange("g r n -> r g n"),
                )

        far = sbuf("far", [P, 2 * W], U8)
        down = sbuf("down", [P, GROUPS * 2 * H], U8)
        weight_raw = sbuf("weight_raw", [P, GROUPS, PACK], BF16)
        weight = sbuf("weight", [P, GROUPS, PACK], F32)
        gain_raw = sbuf("gain_raw", [P, 2, PACK], BF16)
        log_gain_col = sbuf("log_gain_col", [P, 2, PACK], F32)
        log_gain = sbuf("log_gain", [P, W], F32)

        nc.sync.dma_start(out=gain_raw[:], in_=col_gain.rearrange("(b p m) -> p b m", b=2, m=PACK))
        load_rows(0, 0, 1)
        load_near(0, 0)
        load_rows(0, 1, 1)
        load_rows(1, 0, 2)
        load_scales(far_plane, far_scales)
        load_near(1, 0)
        load_rows(2, 0, 2)
        nc.sync.dma_start(out=far[:].bitcast(I32), in_=far_words[0].bitcast(I32))
        load_rows(3, 0, 2)
        nc.sync.dma_start(out=weight_raw[:], in_=row_weight.rearrange("(g p t) -> p g t", p=P, t=PACK))
        load_rows(4, 0, 2)
        for a in range(2):
            load_rows(5 + 2 * a, 0, 2)
            load_rows(6 + 2 * a, 0, 2)
            load_near(a, 1)
        nc.sync.dma_start(
            out=down[:].bitcast(I32).rearrange("p (g n) -> p g n", g=GROUPS),
            in_=down_words.bitcast(I32).rearrange("g p n -> p g n"),
        )
        load_scales(down_plane, down_scales)

        staged, quantised, sums, rounded, result, log_sur = {}, {}, {}, {}, {}, {}

        def stage(key):
            staged[key] = sbuf("staged%d" % turn("staged", STAGED), [P, N, PACK], BF16)
            return staged[key]

        def interleave(key, source):
            nc.vector.tensor_copy(
                out=stage(key)[:].rearrange("p (c i) t -> p c t i", i=4),
                in_=source[:].rearrange("p t (c i) -> p c t i", i=4),
            )

        def quantize(key):
            name = "%s%d_%d" % key
            codes = sbuf("codes_" + name, [P, N], U32)
            scales = sbuf("scales_" + name, [P, N], U8)
            nc.vector.quantize_mx(
                out=codes[:].bitcast(FP8X4), scales=scales[:], in_=staged[key][:].rearrange("p c t -> p (c t)")
            )
            quantised[key] = (codes, scales)

        def sort_words(n):
            sorted_words[n] = sbuf("sorted%d" % turn("sorted", 2), [P, PACK, 2, P], F32)
            nc.vector.tensor_copy(
                out=sorted_words[n][:], in_=unit_rows[n][:].bitcast(F32).rearrange("p j (w u) -> p j u w", u=2)
            )

        def transpose_pair(n, i):
            g, a = divmod(n, PASSES)
            target = stage(("rows", g, a)) if i == 0 else staged["rows", g, a]
            target = target[:].rearrange("p c t -> p (c t)").bitcast(F32)
            target = target.rearrange("p (t j m u) -> p j t m u", t=PACK, j=PACK, u=2)
            bank = psum_bank(turn("turn", TURN_BANKS))
            for j in range(2):
                for u in range(2):
                    if n in SORTED:
                        words = sorted_words[n][:, 2 * i + j, u, :]
                    else:
                        words = pair_rows[2 * g + i, a][:, j, :].bitcast(F32)[:, u : 2 * P : 2]
                    nc.tensor.transpose(bank[:, (2 * j + u) * P : (2 * j + u + 1) * P], words, ident[:])
            nc.scalar.copy(
                out=target[:, 2 * i : 2 * i + 2], in_=bank[:].rearrange("p (j u m t) -> p j t m u", j=2, u=2, t=PACK)
            )

        def spread_log_gain(half):
            bank = psum_bank(TURN_BANKS + half)
            for m in range(PACK):
                column = log_gain_col[:, half, m : m + 1].to_broadcast([P, P])
                nc.tensor.transpose(bank[:, m * P : (m + 1) * P], column, ident[:])
            nc.vector.tensor_copy(
                out=log_gain[:, cols(half)].rearrange("p (n m) -> p n m", m=PACK),
                in_=bank[:].rearrange("p (m n) -> p n m", m=PACK),
            )

        def row_pass(g, t, half, a):
            if a == 0 and half == 0:
                sums[g, t, half] = psum_bank(TURN_BANKS + turn("left", BANKS - TURN_BANKS))
            elif a == 0:
                sums[g, t, half] = psum_bank(turn("late", BANKS))
            codes, scales = quantised["rows", g, a]
            if a < 2:
                rhs, rhs_scale = quantised["near", a, half][0][:].bitcast(FP8X4), quantised["near", a, half][1][:]
            else:
                rhs, rhs_scale = far[:, 2 * N * half : 2 * N * (half + 1)].bitcast(FP4X4), far_plane[:, cols(half)]
            nc.tensor.matmul_mx(
                out=sums[g, t, half][:],
                lhsT=codes[:, t * P : (t + 1) * P].bitcast(FP8X4),
                lhsT_scale=scales[:, t * P : (t + 1) * P],
                rhs=rhs,
                rhs_scale=rhs_scale,
                start=(a == 0),
                stop=(a == PASSES - 1),
            )

        def empty_sums(g, t, half):
            if t == 0:
                rounded[g, half] = sbuf("rounded%d" % turn("rounded", ROUNDED), [P, PACK, N], BF16)
            nc.scalar.activation(
                out=rounded[g, half][:, t, :], in_=sums[g, t, half][:], func=ACT.Copy, scale=weight[:, g, t : t + 1]
            )

        def column_blur(j, half):
            bank = psum_bank(turn("late", BANKS))
            for g in range(GROUPS):
                codes, scales = quantised["h", g, half]
                first = g * H + j * P
                nc.tensor.matmul_mx(
                    out=bank[:],
                    lhsT=down[:, 2 * first : 2 * (first + P)].bitcast(FP4X4),
                    lhsT_scale=down_plane[:, first : first + P],
                    rhs=codes[:].bitcast(FP8X4),
                    rhs_scale=scales[:],
                    start=(g == 0),
                    stop=(g == GROUPS - 1),
                )
            return bank

        to_log = [(i, half) for half in range(2) for i in range(2)]
        to_log.extend([(i, half) for half in range(2) for i in range(2, PAIRS)])
        to_gain = list(to_log)

        def next_log():
            i, half = to_log[0]
            to_log.remove((i, half))
            result[i, half] = sbuf("result%d_%d" % (i, half), [P, 2, N], F32)
            nc.scalar.activation(out=result[i, half][:], in_=pair_rows[i, half], func=ACT.Ln)

        def next_gain():
            i, half = to_gain[0]
            to_gain.remove((i, half))
            nc.vector.tensor_tensor(
                out=result[i, half][:],
                in0=result[i, half][:],
                in1=log_gain[:, cols(half)].unsqueeze(1).to_broadcast([P, 2, N]),
                op=ALU.add,
            )

        def finish(i, half, tiles, columns):
            part = result[i, half][:, tiles, columns]
            nc.vector.tensor_tensor(out=part, in0=part, in1=log_sur[i, half][:, tiles, columns], op=ALU.subtract)
            nc.sync.dma_start(out=out_rows[:, 2 * i : 2 * i + 2, cols(half)][:, tiles, columns], in_=part)

        nc.scalar.activation(out=log_gain_col[:], in_=gain_raw[:], func=ACT.Ln)
        spread_log_gain(0)
        spread_log_gain(1)
        next_log()
        transpose_pair(0, 0)
        next_log()
        interleave(("near", 0, 0), near_raw[0, 0])
        transpose_pair(0, 1)
        next_log()
        quantize(("near", 0, 0))
        quantize(("rows", 0, 0))
        interleave(("near", 1, 0), near_raw[1, 0])
        waiting = [("near", 1, 0)]

        for n in range(UNITS):
            g, a = divmod(n, PASSES)
            if n + 1 < UNITS:
                transpose_pair(n + 1, 0)
                transpose_pair(n + 1, 1)
                if n + 2 in SORTED:
                    sort_words(n + 2)
                quantize(("rows",) + divmod(n + 1, PASSES))
            for key in waiting:
                quantize(key)
            waiting.clear()
            if n == 1:
                nc.vector.tensor_copy(out=weight[:], in_=weight_raw[:])
            if n + 1 == UNITS:
                for first_a in range(PASSES):
                    row_pass(0, 0, 1, first_a)
            for t in range(PACK):
                row_pass(g, t, 0, a)
            if a == 2:
                empty_sums(g, 0, 0)
                empty_sums(g, 1, 0)
            elif a == 0 and g > 0:
                empty_sums(g - 1, 2, 0)
                empty_sums(g - 1, 3, 0)
            else:
                next_log()
            if n + 2 == UNITS:
                next_log()
            if a == 1 and g > 0:
                waiting.append(("h", g - 1, 0))
                interleave(waiting[0], rounded[g - 1, 0])
            elif g == 1:
                waiting.append(("near", a // 2, 1))
                interleave(waiting[0], near_raw[a // 2, 1])
            if g != 1:
                next_gain()
        empty_sums(GROUPS - 1, 2, 0)
        empty_sums(GROUPS - 1, 3, 0)
        interleave(("h", GROUPS - 1, 0), rounded[GROUPS - 1, 0])
        empty_sums(0, 0, 1)
        quantize(("h", GROUPS - 1, 0))

        for g in range(GROUPS):
            for t in range(1 if g == 0 else 0, PACK):
                for a in range(PASSES):
                    row_pass(g, t, 1, a)
                empty_sums(g, t, 1)
            if g == 1:
                next_log()
            interleave(("h", g, 1), rounded[g, 1])
            if g + 1 < GROUPS:
                next_gain()
                quantize(("h", g, 1))
            else:
                quantize(("h", g, 1))
                next_gain()

        order = sorted([(i, half) for i in range(PAIRS) for half in range(2)], key=lambda x: (x[0] + LAG * x[1], x[1]))
        whole = slice(0, N)
        for place, (i, half) in enumerate(order):
            log_sur[i, half] = sbuf("log_sur%d" % turn("log_sur", SURROUND_LOGS), [P, 2, N], F32)
            narrow = place >= len(order) - NARROW
            for j in range(2):
                bank = column_blur(2 * i + j, half)
                very_last = place == len(order) - 1 and j == 1
                for columns in [slice(0, N // 2), slice(N // 2, N)] if very_last else [whole]:
                    nc.scalar.activation(out=log_sur[i, half][:, j, columns], in_=bank[:, columns], func=ACT.Ln)
                    if narrow:
                        finish(i, half, slice(j, j + 1), columns)
            if not narrow:
                finish(i, half, slice(0, 2), whole)
            if place % 2 == 0 and to_log:
                next_log()
            elif to_gain:
                next_gain()
